import numpy as np
import ml_dtypes


def mxq(x, axis, fmt="e4m3"):
    dtype, down = {"e4m3": (ml_dtypes.float8_e4m3fn, 7), "e5m2": (ml_dtypes.float8_e5m2, 14)}[fmt]
    v = np.moveaxis(np.asarray(x, np.float32).astype(ml_dtypes.bfloat16).astype(np.float64), axis, -1)
    blocks = v.reshape(v.shape[:-1] + (-1, 32))
    amax = np.abs(blocks).max(-1, keepdims=True)
    byte = np.maximum(np.where(amax > 0, np.frexp(amax)[1] - 1 + 127, 0) - down, 1)
    scale = np.exp2(byte - 127.0)
    codes = (blocks / scale).astype(np.float32).astype(dtype).astype(np.float64)
    return np.moveaxis((codes * scale).reshape(v.shape), -1, axis)


WIDE = False


def mx_kscale(k):
    if not WIDE:
        return np.ones(k)
    levels = np.array([10, -10, 5, -5, 0])
    if k % 512:
        return np.exp2(np.random.permutation(np.resize(levels, k // 32))).repeat(32)
    a = np.empty((k // 512, 16))
    for p in range(k // 512):
        a[p, :8] = np.random.permutation(np.resize(levels, 8))
        for g in range(8):
            far = levels[np.abs(levels - a[p, g]) >= 10]
            a[p, g + 8] = far[np.random.randint(len(far))]
    return np.exp2(a.ravel()).repeat(32)


def f64(x):
    return np.asarray(x).astype(np.float64)


def striped(idx):
    return np.tile(idx.reshape(-1, 16).T, (8, 1)).astype(np.uint16)


def unstriped(offs):
    return offs[:16].T.reshape(-1).astype(np.int64)


def pack_weight(w):
    k, n = w.shape
    w = f64(np.asarray(w, np.float32).astype(ml_dtypes.bfloat16)).reshape(k // 32, 32, n)
    amax = np.abs(w).max(1)
    byte = np.clip(np.where(amax > 0, np.frexp(amax)[1] - 1 + 127 - 7, 1), 1, 254)
    scaled = (w * np.exp2(127.0 - byte)[:, None, :]).reshape(k, n).astype(np.float32)
    words = np.ascontiguousarray(scaled.reshape(k // 512, 128, 4, n).transpose(0, 1, 3, 2)).astype(ml_dtypes.float8_e4m3fn).view(np.uint8)
    return words, np.ascontiguousarray(byte.astype(np.uint8).reshape(k // 512, 16, n))


def unpack_weight(words, scales):
    g, p, n, _ = words.shape
    vals = np.ascontiguousarray(words).view(ml_dtypes.float8_e4m3fn).astype(np.float64) * np.repeat(np.exp2(scales.astype(np.float64) - 127.0), 8, axis=1)[..., None]
    return vals.transpose(0, 1, 3, 2).reshape(g * 512, n)


def relu(v):
    return np.maximum(v, 0.0)


def sigmoid(v):
    return 1.0 / (1.0 + np.exp(-np.maximum(v, -700.0)))


K, T, S, D, H, V, Z, W = 512, 2048, 512, 2, 512, 256, 512, 2048
P = 2 ** 7


def setup_inputs():
    n = np.random.standard_normal
    s = mx_kscale(K)[:, None]
    packed_xT = pack_weight(n((K, T)) * s)
    packed_eT = pack_weight(n((K, W)) * s)
    return {
        "x_words": packed_xT[0],
        "x_scales": packed_xT[1],
        "w1": (n((K, H)) / np.sqrt(K) / s).astype(np.float32),
        "w2": (n((K, H)) / np.sqrt(K) / s).astype(np.float32),
        "e_words": packed_eT[0],
        "e_scales": packed_eT[1],
        "unit": (np.random.uniform(0.6, 1.4, (K, 1)) / np.sqrt(K) / s).astype(np.float32),
        "age": (np.tile(np.random.uniform(0.1, 1.5, W), (P, 1))).astype(np.float32),
        "offs": striped(np.random.permutation(T)[:S]),
        "prv": striped(np.random.permutation(S)),
        "art": striped(np.random.permutation(W)[:Z]),
        "mt": striped(np.random.permutation(V)),
        "dup": striped(np.random.permutation(Z)),
    }


def reference(x_words, x_scales, w1, w2, e_words, e_scales, unit, age, offs, prv, art, mt, dup):
    xq = unpack_weight(x_words, x_scales)[:, unstriped(offs)]
    y = mxq(f64(w1), 0, "e4m3").T @ xq
    yp = y[:, unstriped(prv)]
    nov = y - (0.5 * yp)
    yt = mxq(f64(w2), 0, "e4m3").T @ xq
    dw = nov * sigmoid(yt)
    int_ = dw.reshape(len(dw), -1, D).sum(axis=2)
    soc = np.maximum(int_, 0.8 * int_[:, unstriped(mt)])
    hid = f64(unit) * soc
    e_art = unpack_weight(e_words, e_scales)[:, unstriped(art)]
    sc = mxq(hid, 0, "e4m3").T @ e_art
    fr = sc * (np.exp(-1.0 * (f64(age)[:1][:, unstriped(art)])))
    fd = fr[:, unstriped(dup)]
    return fr - relu(fd)

@@ -1,0 +1,228 @@
+from contextlib import ExitStack
+
+import concourse.mybir as mybir
+
+K, T, S, H, V = 512, 2048, 512, 512, 256
+FLOPS = 2 * K * H * S * 2 + 2 * H * V * S
+
+F32 = mybir.dt.float32
+BF16 = mybir.dt.bfloat16
+I32 = mybir.dt.int32
+U32 = mybir.dt.uint32
+U16 = mybir.dt.uint16
+U8 = mybir.dt.uint8
+FP8X4 = mybir.dt.float8_e4m3fn_x4
+ALU = mybir.AluOpType
+ACT = mybir.ActivationFunctionType
+
+P = 128
+PACK = 4
+LIST_COL = 16
+
+
+def tile_picked_ynewsfd_dup_p_kernel(
+    tc, x_words, x_scales, w1, w2, e_words, e_scales, unit, age, offs, prv, art, mt, dup, out
+):
+    nc = tc.nc
+    with ExitStack() as ctx:
+        lists = ctx.enter_context(tc.tile_pool(name="lists", bufs=1))
+        sb = ctx.enter_context(tc.tile_pool(name="sb", bufs=1))
+        psum = ctx.enter_context(tc.psum_pool(name="psum", bufs=1))
+
+        def load_list(src, name):
+            tile = lists.tile([P, src.shape[1]], U16, name=name)
+            nc.sync.dma_start(tile[:], src)
+            return tile
+
+        def entries(tile, first, count):
+            return tile[:, first // LIST_COL : (first + count) // LIST_COL]
+
+        def load_words(src, name):
+            tile = sb.tile([P, T], U32, name=name)
+            nc.sync.dma_start(tile[:].bitcast(I32), src[0].rearrange("p n t -> p (n t)").bitcast(I32))
+            return tile
+
+        def load_scales(src, name, queue):
+            tile = sb.tile([P, T], U8, name=name)
+            nc.vector.memset(tile[:].bitcast(I32), 0)
+            for q in range(4):
+                queue.dma_start(
+                    tile[32 * q : 32 * q + 4, :].bitcast(I32), src[0, 4 * q : 4 * q + 4, :].bitcast(I32)
+                )
+            return tile
+
+        def load_scales_staged(src, name):
+            rows = sb.tile([P, T // 4], I32, name=name + "_rows")
+            tile = sb.tile([P, T], U8, name=name)
+            nc.vector.memset(tile[:].bitcast(I32), 0)
+            for q in range(4):
+                (nc.sync, nc.scalar, nc.scalar, nc.scalar)[q].dma_start(rows[32 * q : 32 * q + 4, :], src[0, 4 * q : 4 * q + 4, :].bitcast(I32))
+            for q in range(4):
+                nc.vector.tensor_copy(tile[32 * q : 32 * q + 4, :].bitcast(I32), rows[32 * q : 32 * q + 4, :])
+            return tile
+
+        def load_weight(src, name):
+            rows = src.rearrange("(p j) c -> p j c", j=PACK)
+            parts = []
+            for h in range(2):
+                raw = sb.tile([P, PACK, H // 2], F32, name="%s_raw%d" % (name, h))
+                nc.sync.dma_start(raw[:], rows[:, :, h * (H // 2) : (h + 1) * (H // 2)])
+                parts.append(raw)
+            return parts
+
+        def gather(dtype, window, offsets, name, tag):
+            picked = sb.tile([P, S], dtype, name=name, tag=tag, align_bytes=64)
+            nc.vector.tensor_copy(picked[:], window[:].indirect(offsets[:]))
+            return picked
+
+        def deal_weight(parts, name, copies):
+            dealt = sb.tile([P, PACK, P, PACK], BF16, name=name, tag="dealt", align_bytes=64)
+            for h in range(2):
+                copies[h](
+                    dealt[:].rearrange("p t m j -> p m j t")[:, h * 64 : (h + 1) * 64],
+                    parts[h][:].rearrange("p j (m t) -> p m j t", t=PACK),
+                )
+            return dealt
+
+        def quantize(values, width, name):
+            codes = sb.tile([P, width], U32, name=name + "_codes", align_bytes=64)
+            scales = sb.tile([P, width], U8, name=name + "_scales", align_bytes=64)
+            nc.vector.quantize_mx(out=codes[:].bitcast(FP8X4), scales=scales[:], in_=values)
+            return codes, scales
+
+        def product(stationary, moving, tag):
+            acc = psum.tile([P, S], F32, name=tag, tag=tag)
+            nc.tensor.matmul_mx(
+                out=acc[:],
+                lhsT=stationary[0][:].bitcast(FP8X4),
+                lhsT_scale=stationary[1][:],
+                rhs=moving[0][:].bitcast(FP8X4),
+                rhs_scale=moving[1][:],
+                start=True,
+                stop=True,
+            )
+            return acc
+
+        offs_t = load_list(offs, "offs_t")
+        xs = load_scales_staged(x_scales, "xs")
+        xw = load_words(x_words, "xw")
+        w1_raw = load_weight(w1, "w1")
+        prv_t = load_list(prv, "prv_t")
+        w2_raw = load_weight(w2, "w2")
+        ew = load_words(e_words, "ew")
+        es = load_scales(e_scales, "es", nc.sync)
+        art_t = load_list(art, "art_t")
+        mt_t = load_list(mt, "mt_t")
+        unit_t = sb.tile([P, PACK], F32, name="unit_t")
+        nc.sync.dma_start(unit_t[:], unit.rearrange("(p t) o -> p (t o)", t=PACK))
+        age_t = sb.tile([P, T], F32, name="age_t")
+        nc.sync.dma_start(age_t[:], age)
+        dup_t = load_list(dup, "dup_t")
+
+        xq_scales = gather(U8, xs, offs_t, "xq_scales", "xq_scales")
+        xq_words = gather(U32, xw, offs_t, "xq_words", "xq_words")
+        xq = (xq_words, xq_scales)
+        w1_dealt = deal_weight(w1_raw, "w1_dealt", (nc.scalar.copy, nc.vector.tensor_copy))
+        y_ps = []
+        for t in range(PACK):
+            wq = quantize(w1_dealt[:, t].rearrange("p m j -> p (m j)"), P, "w1q%d" % t)
+            y_ps.append(product(wq, xq, "bank%d" % t))
+        w2_dealt = deal_weight(w2_raw, "w2_dealt", (nc.vector.tensor_copy, nc.vector.tensor_copy))
+        yt_ps = []
+        for t in range(PACK):
+            wq = quantize(w2_dealt[:, t].rearrange("p m j -> p (m j)"), P, "w2q%d" % t)
+            yt_ps.append(product(wq, xq, "bank%d" % (PACK + t)))
+
+        y_sb, yp, th, nov, interest = {}, {}, {}, {}, {}
+        hid_planes = sb.tile([P, PACK, V], BF16, name="hid_planes")
+
+        def fetch_previous(t):
+            y_sb[t] = sb.tile([P, S], F32, name="y%d" % t)
+            nc.scalar.copy(y_sb[t][:], y_ps[t][:])
+            yp[t] = sb.tile([P, S], F32, name="yp%d" % t)
+            for h in range(2):
+                nc.scalar.activation(
+                    yp[t][:, h * 256 : (h + 1) * 256], y_sb[t][:].indirect(entries(prv_t, h * 256, 256)), ACT.Copy
+                )
+
+        def gate(t):
+            th[t] = sb.tile([P, S], F32, name="th%d" % t)
+            nc.scalar.activation(th[t][:], yt_ps[t][:], ACT.Tanh, scale=0.5)
+
+        def novelty(t):
+            nov[t] = sb.tile([P, S], F32, name="nov%d" % t)
+            nc.vector.scalar_tensor_tensor(nov[t][:], yp[t][:], -0.5, y_sb[t][:], ALU.mult, ALU.add)
+
+        def gated_sum(t):
+            dw = sb.tile([P, V, 2], F32, name="dw%d" % t, tag="dw%d" % t, align_bytes=64)
+            nc.vector.scalar_tensor_tensor(
+                dw[:].rearrange("p v d -> p (v d)"), th[t][:], 1.0, nov[t][:], ALU.add, ALU.mult
+            )
+            interest[t] = sb.tile([P, V], F32, name="interest%d" % t)
+            nc.vector.tensor_tensor(interest[t][:], dw[:, :, 0], dw[:, :, 1], ALU.add)
+
+        def compete(t):
+            mate = sb.tile([P, V], F32, name="mate%d" % t)
+            for h in range(2):
+                nc.scalar.activation(
+                    mate[:, h * P : (h + 1) * P], interest[t][:].indirect(entries(mt_t, h * P, P)), ACT.Copy
+                )
+            soc = sb.tile([P, V], F32, name="soc%d" % t)
+            nc.vector.scalar_tensor_tensor(soc[:], mate[:], 0.8, interest[t][:], ALU.mult, ALU.max)
+            nc.vector.tensor_scalar(hid_planes[:, t, :], soc[:], unit_t[:, t : t + 1], 0.5, ALU.mult, ALU.mult)
+
+        fetch_previous(0)
+        gate(0)
+        novelty(0)
+        gated_sum(0)
+        fetch_previous(1)
+        gate(1)
+        novelty(1)
+        gated_sum(1)
+        compete(0)
+        eq_scales = gather(U8, es, art_t, "eq_scales", "dw1")
+        fetch_previous(2)
+        gate(2)
+        novelty(2)
+        gated_sum(2)
+        compete(1)
+        eq_words = gather(U32, ew, art_t, "eq_words", "dw2")
+        fetch_previous(3)
+        gate(3)
+        novelty(3)
+        gated_sum(3)
+        compete(2)
+        compete(3)
+        eq = (eq_words, eq_scales)
+        fade = sb.tile([P, S], F32, name="fade", tag="dw3", align_bytes=64)
+        nc.scalar.activation(fade[:], age_t[:].indirect(art_t[:]), ACT.Exp, scale=-1.0)
+
+        grouped = []
+        for h in range(2):
+            g = sb.tile([P, P, PACK], BF16, name="hid_grouped%d" % h, align_bytes=64)
+            nc.vector.tensor_copy(
+                g[:].rearrange("p (c i) t -> p c t i", i=4),
+                hid_planes[:, :, h * P : (h + 1) * P].rearrange("p t (c i) -> p c t i", i=4),
+            )
+            grouped.append(g)
+        sc = []
+        for h in range(2):
+            hq = quantize(grouped[h][:].rearrange("p v t -> p (v t)"), P, "hq%d" % h)
+            sc.append(product(hq, eq, "bank%d" % h))
+        neg = []
+        for h in range(2):
+            n = sb.tile([P, S], F32, name="neg%d" % h)
+            nc.vector.scalar_tensor_tensor(n[:], sc[h][:], -1.0, fade[:], ALU.mult, ALU.mult)
+            neg.append(n)
+        for h in range(2):
+            for c in range(2):
+                twin = sb.tile([P, 256], F32, name="twin%d%d" % (h, c))
+                window = neg[h][:].indirect(entries(dup_t, c * 256, 256))
+                if h == 1 and c == 0:
+                    nc.vector.tensor_copy(twin[:], window)
+                else:
+                    nc.scalar.activation(twin[:], window, ACT.Copy)
+                res = sb.tile([P, 256], F32, name="res%d%d" % (h, c))
+                cols = slice(c * 256, (c + 1) * 256)
+                nc.vector.scalar_tensor_tensor(res[:], twin[:], 0.0, neg[h][:, cols], ALU.min, ALU.subtract)
+                nc.sync.dma_start(out[h * P : (h + 1) * P, cols], res[:])

@@ -56,7 +56,7 @@ def tile_picked_ynewsfd_dup_p_kernel(
             tile = sb.tile([P, T], U8, name=name)
             nc.vector.memset(tile[:].bitcast(I32), 0)
             for q in range(4):
-                (nc.sync, nc.scalar, nc.scalar, nc.scalar)[q].dma_start(rows[32 * q : 32 * q + 4, :], src[0, 4 * q : 4 * q + 4, :].bitcast(I32))
+                (nc.sync, nc.sync, nc.scalar, nc.scalar)[q].dma_start(rows[32 * q : 32 * q + 4, :], src[0, 4 * q : 4 * q + 4, :].bitcast(I32))
             for q in range(4):
                 nc.vector.tensor_copy(tile[32 * q : 32 * q + 4, :].bitcast(I32), rows[32 * q : 32 * q + 4, :])
             return tile
@@ -76,7 +76,7 @@ def tile_picked_ynewsfd_dup_p_kernel(
             return picked
 
         def deal_weight(parts, name, copies):
-            dealt = sb.tile([P, PACK, P, PACK], BF16, name=name, tag="dealt", align_bytes=64)
+            dealt = sb.tile([P, PACK, P, PACK], BF16, name=name, tag=name, align_bytes=64)
             for h in range(2):
                 copies[h](
                     dealt[:].rearrange("p t m j -> p m j t")[:, h * 64 : (h + 1) * 64],
@@ -90,12 +90,20 @@ def tile_picked_ynewsfd_dup_p_kernel(
             nc.vector.quantize_mx(out=codes[:].bitcast(FP8X4), scales=scales[:], in_=values)
             return codes, scales
 
+        def quantize_planes(dealt, name):
+            first = quantize(dealt[:, 0].rearrange("p m j -> p (m j)"), P, name + "a")
+            rest = quantize(dealt[:, 1:].rearrange("p t m j -> p (t m j)"), 3 * P, name + "b")
+            planes = [(first[0][:], first[1][:])]
+            for t in range(3):
+                planes.append((rest[0][:, t * P : (t + 1) * P], rest[1][:, t * P : (t + 1) * P]))
+            return planes
+
         def product(stationary, moving, tag):
             acc = psum.tile([P, S], F32, name=tag, tag=tag)
             nc.tensor.matmul_mx(
                 out=acc[:],
-                lhsT=stationary[0][:].bitcast(FP8X4),
-                lhsT_scale=stationary[1][:],
+                lhsT=stationary[0].bitcast(FP8X4),
+                lhsT_scale=stationary[1],
                 rhs=moving[0][:].bitcast(FP8X4),
                 rhs_scale=moving[1][:],
                 start=True,
@@ -109,9 +117,9 @@ def tile_picked_ynewsfd_dup_p_kernel(
         w1_raw = load_weight(w1, "w1")
         prv_t = load_list(prv, "prv_t")
         w2_raw = load_weight(w2, "w2")
-        ew = load_words(e_words, "ew")
-        es = load_scales(e_scales, "es", nc.sync)
         art_t = load_list(art, "art_t")
+        es = load_scales(e_scales, "es", nc.sync)
+        ew = load_words(e_words, "ew")
         mt_t = load_list(mt, "mt_t")
         unit_t = sb.tile([P, PACK], F32, name="unit_t")
         nc.sync.dma_start(unit_t[:], unit.rearrange("(p t) o -> p (t o)", t=PACK))
@@ -123,27 +131,30 @@ def tile_picked_ynewsfd_dup_p_kernel(
         xq_words = gather(U32, xw, offs_t, "xq_words", "xq_words")
         xq = (xq_words, xq_scales)
         w1_dealt = deal_weight(w1_raw, "w1_dealt", (nc.scalar.copy, nc.vector.tensor_copy))
-        y_ps = []
-        for t in range(PACK):
-            wq = quantize(w1_dealt[:, t].rearrange("p m j -> p (m j)"), P, "w1q%d" % t)
-            y_ps.append(product(wq, xq, "bank%d" % t))
-        w2_dealt = deal_weight(w2_raw, "w2_dealt", (nc.vector.tensor_copy, nc.vector.tensor_copy))
-        yt_ps = []
-        for t in range(PACK):
-            wq = quantize(w2_dealt[:, t].rearrange("p m j -> p (m j)"), P, "w2q%d" % t)
-            yt_ps.append(product(wq, xq, "bank%d" % (PACK + t)))
+        w1_planes = quantize_planes(w1_dealt, "w1q")
+        y_ps = {t: product(w1_planes[t], xq, "bank%d" % t) for t in range(2)}
+        w2_dealt = deal_weight(w2_raw, "w2_dealt", (nc.scalar.copy, nc.vector.tensor_copy))
+        w2_planes = quantize_planes(w2_dealt, "w2q")
+        yt_ps = [product(w2_planes[t], xq, "bank%d" % (2 + t)) for t in range(PACK)]
 
         y_sb, yp, th, nov, interest = {}, {}, {}, {}, {}
         hid_planes = sb.tile([P, PACK, V], BF16, name="hid_planes")
 
+        def window_tile(width, spare, name):
+            tile = sb.tile([P, width + spare], F32, name=name)
+            nc.gpsimd.memset(tile[:, width:], 0.0)
+            return tile
+
+        def keep_y(t, on_vector):
+            y_sb[t] = window_tile(S, 8, "y%d" % t)
+            if on_vector:
+                nc.vector.tensor_scalar(y_sb[t][:, :S], y_ps[t][:], 0.5, None, ALU.mult)
+            else:
+                nc.scalar.activation(y_sb[t][:, :S], y_ps[t][:], ACT.Copy, scale=0.5)
+
         def fetch_previous(t):
-            y_sb[t] = sb.tile([P, S], F32, name="y%d" % t)
-            nc.scalar.copy(y_sb[t][:], y_ps[t][:])
-            yp[t] = sb.tile([P, S], F32, name="yp%d" % t)
-            for h in range(2):
-                nc.scalar.activation(
-                    yp[t][:, h * 256 : (h + 1) * 256], y_sb[t][:].indirect(entries(prv_t, h * 256, 256)), ACT.Copy
-                )
+            yp[t] = sb.tile([P, S], F32, name="yp%d" % t, tag="yp%d" % t, align_bytes=64)
+            nc.scalar.activation(yp[t][:], y_sb[t][:].indirect(prv_t[:]), ACT.Copy)
 
         def gate(t):
             th[t] = sb.tile([P, S], F32, name="th%d" % t)
@@ -151,52 +162,74 @@ def tile_picked_ynewsfd_dup_p_kernel(
 
         def novelty(t):
             nov[t] = sb.tile([P, S], F32, name="nov%d" % t)
-            nc.vector.scalar_tensor_tensor(nov[t][:], yp[t][:], -0.5, y_sb[t][:], ALU.mult, ALU.add)
+            nc.vector.scalar_tensor_tensor(nov[t][:], yp[t][:], -0.5, y_sb[t][:, :S], ALU.mult, ALU.add)
 
-        def gated_sum(t):
-            dw = sb.tile([P, V, 2], F32, name="dw%d" % t, tag="dw%d" % t, align_bytes=64)
+        def gated(t):
+            dw[t] = sb.tile([P, V, 2], F32, name="dw%d" % t, tag="dw%d" % t, align_bytes=64)
             nc.vector.scalar_tensor_tensor(
-                dw[:].rearrange("p v d -> p (v d)"), th[t][:], 1.0, nov[t][:], ALU.add, ALU.mult
+                dw[t][:].rearrange("p v d -> p (v d)"), th[t][:], 1.0, nov[t][:], ALU.add, ALU.mult
             )
-            interest[t] = sb.tile([P, V], F32, name="interest%d" % t)
-            nc.vector.tensor_tensor(interest[t][:], dw[:, :, 0], dw[:, :, 1], ALU.add)
 
-        def compete(t):
-            mate = sb.tile([P, V], F32, name="mate%d" % t)
-            for h in range(2):
-                nc.scalar.activation(
-                    mate[:, h * P : (h + 1) * P], interest[t][:].indirect(entries(mt_t, h * P, P)), ACT.Copy
-                )
-            soc = sb.tile([P, V], F32, name="soc%d" % t)
-            nc.vector.scalar_tensor_tensor(soc[:], mate[:], 0.8, interest[t][:], ALU.mult, ALU.max)
-            nc.vector.tensor_scalar(hid_planes[:, t, :], soc[:], unit_t[:, t : t + 1], 0.5, ALU.mult, ALU.mult)
+        def pair_sum(t):
+            interest[t] = window_tile(V, 8, "interest%d" % t)
+            nc.vector.tensor_tensor(interest[t][:, :V], dw[t][:, :, 0], dw[t][:, :, 1], ALU.add)
 
+        def fetch_mate(t, first, count):
+            mate[t, first] = sb.tile([P, count], F32, name="mate%d_%d" % (t, first))
+            nc.scalar.activation(mate[t, first][:], interest[t][:].indirect(entries(mt_t, first, count)), ACT.Copy)
+
+        def compete(t, first, count):
+            soc[t, first] = sb.tile([P, count], F32, name="soc%d_%d" % (t, first))
+            nc.vector.scalar_tensor_tensor(
+                soc[t, first][:], mate[t, first][:], 0.8, interest[t][:, first : first + count], ALU.mult, ALU.max
+            )
+
+        dw, mate, soc = {}, {}, {}
+        eq_scales = gather(U8, es, art_t, "eq_scales", "w2_dealt")
+        keep_y(0, False)
         fetch_previous(0)
-        gate(0)
         novelty(0)
-        gated_sum(0)
+        eq_words = gather(U32, ew, art_t, "eq_words", "yp0")
+        keep_y(1, False)
         fetch_previous(1)
-        gate(1)
         novelty(1)
-        gated_sum(1)
-        compete(0)
-        eq_scales = gather(U8, es, art_t, "eq_scales", "dw1")
+        gate(0)
+        y_ps[2] = product(w1_planes[2], xq, "bank2")
+        gate(1)
+        y_ps[3] = product(w1_planes[3], xq, "bank3")
+        gated(0)
+        gated(1)
+        pair_sum(0)
+        pair_sum(1)
+        keep_y(2, False)
         fetch_previous(2)
+        keep_y(3, True)
         gate(2)
-        novelty(2)
-        gated_sum(2)
-        compete(1)
-        eq_words = gather(U32, ew, art_t, "eq_words", "dw2")
         fetch_previous(3)
         gate(3)
+        novelty(2)
+        gated(2)
         novelty(3)
-        gated_sum(3)
-        compete(2)
-        compete(3)
-        eq = (eq_words, eq_scales)
+        pair_sum(2)
+        gated(3)
+        pair_sum(3)
+        for t in range(3):
+            fetch_mate(t, 0, V)
+        for h in range(2):
+            fetch_mate(3, h * P, P)
+        for t in range(3):
+            compete(t, 0, V)
+        for h in range(2):
+            compete(3, h * P, P)
+        for h in range(2):
+            nc.vector.tensor_scalar(
+                hid_planes[:, 3, h * P : (h + 1) * P], soc[3, h * P][:], unit_t[:, 3:4], None, ALU.mult
+            )
+        for t in range(3):
+            nc.scalar.activation(hid_planes[:, t, :], soc[t, 0][:], ACT.Copy, scale=unit_t[:, t : t + 1])
         fade = sb.tile([P, S], F32, name="fade", tag="dw3", align_bytes=64)
         nc.scalar.activation(fade[:], age_t[:].indirect(art_t[:]), ACT.Exp, scale=-1.0)
-
+        eq = (eq_words, eq_scales)
         grouped = []
         for h in range(2):
             g = sb.tile([P, P, PACK], BF16, name="hid_grouped%d" % h, align_bytes=64)
@@ -208,7 +241,7 @@ def tile_picked_ynewsfd_dup_p_kernel(
         sc = []
         for h in range(2):
             hq = quantize(grouped[h][:].rearrange("p v t -> p (v t)"), P, "hq%d" % h)
-            sc.append(product(hq, eq, "bank%d" % h))
+            sc.append(product((hq[0][:], hq[1][:]), eq, "bank%d" % h))
         neg = []
         for h in range(2):
             n = sb.tile([P, S], F32, name="neg%d" % h)

@@ -75,12 +75,13 @@ def tile_picked_ynewsfd_dup_p_kernel(
             nc.vector.tensor_copy(picked[:], window[:].indirect(offsets[:]))
             return picked
 
-        def deal_weight(parts, name, copies):
-            dealt = sb.tile([P, PACK, P, PACK], BF16, name=name, tag=name, align_bytes=64)
-            for h in range(2):
-                copies[h](
-                    dealt[:].rearrange("p t m j -> p m j t")[:, h * 64 : (h + 1) * 64],
-                    parts[h][:].rearrange("p j (m t) -> p m j t", t=PACK),
+        def deal_weight(parts, name, shares):
+            dealt = sb.tile([P, PACK, P, PACK], BF16, name=name, tag="dealt", align_bytes=64)
+            for copy, first, last in shares:
+                h = first // 64
+                copy(
+                    dealt[:].rearrange("p t m j -> p m j t")[:, first:last],
+                    parts[h][:].rearrange("p j (m t) -> p m j t", t=PACK)[:, first - 64 * h : last - 64 * h],
                 )
             return dealt
 
@@ -130,15 +131,14 @@ def tile_picked_ynewsfd_dup_p_kernel(
         xq_scales = gather(U8, xs, offs_t, "xq_scales", "xq_scales")
         xq_words = gather(U32, xw, offs_t, "xq_words", "xq_words")
         xq = (xq_words, xq_scales)
-        w1_dealt = deal_weight(w1_raw, "w1_dealt", (nc.scalar.copy, nc.vector.tensor_copy))
+        w1_dealt = deal_weight(w1_raw, "w1_dealt", ((nc.scalar.copy, 0, 64), (nc.vector.tensor_copy, 64, 104), (nc.scalar.copy, 104, 128)))
         w1_planes = quantize_planes(w1_dealt, "w1q")
         y_ps = {t: product(w1_planes[t], xq, "bank%d" % t) for t in range(2)}
-        w2_dealt = deal_weight(w2_raw, "w2_dealt", (nc.scalar.copy, nc.vector.tensor_copy))
+        w2_dealt = deal_weight(w2_raw, "w2_dealt", ((nc.vector.tensor_copy, 0, 64), (nc.vector.tensor_copy, 64, 128)))
         w2_planes = quantize_planes(w2_dealt, "w2q")
         yt_ps = [product(w2_planes[t], xq, "bank%d" % (2 + t)) for t in range(PACK)]
 
         y_sb, yp, th, nov, interest = {}, {}, {}, {}, {}
-        hid_planes = sb.tile([P, PACK, V], BF16, name="hid_planes")
 
         def window_tile(width, spare, name):
             tile = sb.tile([P, width + spare], F32, name=name)
@@ -157,7 +157,7 @@ def tile_picked_ynewsfd_dup_p_kernel(
             nc.scalar.activation(yp[t][:], y_sb[t][:].indirect(prv_t[:]), ACT.Copy)
 
         def gate(t):
-            th[t] = sb.tile([P, S], F32, name="th%d" % t)
+            th[t] = sb.tile([P, S], F32, name="th%d" % t, tag="th%d" % t, align_bytes=64)
             nc.scalar.activation(th[t][:], yt_ps[t][:], ACT.Tanh, scale=0.5)
 
         def novelty(t):
@@ -178,14 +178,14 @@ def tile_picked_ynewsfd_dup_p_kernel(
             mate[t, first] = sb.tile([P, count], F32, name="mate%d_%d" % (t, first))
             nc.scalar.activation(mate[t, first][:], interest[t][:].indirect(entries(mt_t, first, count)), ACT.Copy)
 
-        def compete(t, first, count):
-            soc[t, first] = sb.tile([P, count], F32, name="soc%d_%d" % (t, first))
+        def compete(t, first, count, tag):
+            soc[t, first] = sb.tile([P, count], F32, name="soc%d_%d" % (t, first), tag=tag, align_bytes=64)
             nc.vector.scalar_tensor_tensor(
                 soc[t, first][:], mate[t, first][:], 0.8, interest[t][:, first : first + count], ALU.mult, ALU.max
             )
 
         dw, mate, soc = {}, {}, {}
-        eq_scales = gather(U8, es, art_t, "eq_scales", "w2_dealt")
+        eq_scales = gather(U8, es, art_t, "eq_scales", "dealt")
         keep_y(0, False)
         fetch_previous(0)
         novelty(0)
@@ -199,11 +199,11 @@ def tile_picked_ynewsfd_dup_p_kernel(
         y_ps[3] = product(w1_planes[3], xq, "bank3")
         gated(0)
         gated(1)
+        keep_y(3, True)
         pair_sum(0)
         pair_sum(1)
         keep_y(2, False)
         fetch_previous(2)
-        keep_y(3, True)
         gate(2)
         fetch_previous(3)
         gate(3)
@@ -213,21 +213,23 @@ def tile_picked_ynewsfd_dup_p_kernel(
         pair_sum(2)
         gated(3)
         pair_sum(3)
+        hid_planes = sb.tile([P, PACK, V], BF16, name="hid_planes", tag="dw3", align_bytes=64)
         for t in range(3):
             fetch_mate(t, 0, V)
         for h in range(2):
             fetch_mate(3, h * P, P)
         for t in range(3):
-            compete(t, 0, V)
+            compete(t, 0, V, ("yp2", "yp3", "th3")[t])
         for h in range(2):
-            compete(3, h * P, P)
+            compete(3, h * P, P, "soc3%d" % h)
         for h in range(2):
             nc.vector.tensor_scalar(
                 hid_planes[:, 3, h * P : (h + 1) * P], soc[3, h * P][:], unit_t[:, 3:4], None, ALU.mult
             )
-        for t in range(3):
+        nc.vector.tensor_scalar(hid_planes[:, 2, :], soc[2, 0][:], unit_t[:, 2:3], None, ALU.mult)
+        for t in range(2):
             nc.scalar.activation(hid_planes[:, t, :], soc[t, 0][:], ACT.Copy, scale=unit_t[:, t : t + 1])
-        fade = sb.tile([P, S], F32, name="fade", tag="dw3", align_bytes=64)
+        fade = sb.tile([P, S], F32, name="fade", tag="yp2", align_bytes=64)
         nc.scalar.activation(fade[:], age_t[:].indirect(art_t[:]), ACT.Exp, scale=-1.0)
         eq = (eq_words, eq_scales)
         grouped = []

@@ -220,29 +220,25 @@ def tile_picked_ynewsfd_dup_p_kernel(
             fetch_mate(3, h * P, P)
         for t in range(3):
             compete(t, 0, V, ("yp2", "yp3", "th3")[t])
-        for h in range(2):
-            compete(3, h * P, P, "soc3%d" % h)
-        for h in range(2):
-            nc.vector.tensor_scalar(
-                hid_planes[:, 3, h * P : (h + 1) * P], soc[3, h * P][:], unit_t[:, 3:4], None, ALU.mult
-            )
         nc.vector.tensor_scalar(hid_planes[:, 2, :], soc[2, 0][:], unit_t[:, 2:3], None, ALU.mult)
         for t in range(2):
             nc.scalar.activation(hid_planes[:, t, :], soc[t, 0][:], ACT.Copy, scale=unit_t[:, t : t + 1])
         fade = sb.tile([P, S], F32, name="fade", tag="yp2", align_bytes=64)
         nc.scalar.activation(fade[:], age_t[:].indirect(art_t[:]), ACT.Exp, scale=-1.0)
-        eq = (eq_words, eq_scales)
-        grouped = []
         for h in range(2):
+            compete(3, h * P, P, "soc3%d" % h)
+        eq = (eq_words, eq_scales)
+        sc = []
+        for h in range(2):
+            nc.vector.tensor_scalar(
+                hid_planes[:, 3, h * P : (h + 1) * P], soc[3, h * P][:], unit_t[:, 3:4], None, ALU.mult
+            )
             g = sb.tile([P, P, PACK], BF16, name="hid_grouped%d" % h, align_bytes=64)
             nc.vector.tensor_copy(
                 g[:].rearrange("p (c i) t -> p c t i", i=4),
                 hid_planes[:, :, h * P : (h + 1) * P].rearrange("p t (c i) -> p c t i", i=4),
             )
-            grouped.append(g)
-        sc = []
-        for h in range(2):
-            hq = quantize(grouped[h][:].rearrange("p v t -> p (v t)"), P, "hq%d" % h)
+            hq = quantize(g[:].rearrange("p v t -> p (v t)"), P, "hq%d" % h)
             sc.append(product((hq[0][:], hq[1][:]), eq, "bank%d" % h))
         neg = []
         for h in range(2):

from contextlib import ExitStack

import concourse.mybir as mybir

K, T, S, H, V = 512, 2048, 512, 512, 256
FLOPS = 2 * K * H * S * 2 + 2 * H * V * S

F32 = mybir.dt.float32
BF16 = mybir.dt.bfloat16
I32 = mybir.dt.int32
U32 = mybir.dt.uint32
U16 = mybir.dt.uint16
U8 = mybir.dt.uint8
FP8X4 = mybir.dt.float8_e4m3fn_x4
ALU = mybir.AluOpType
ACT = mybir.ActivationFunctionType

P = 128
PACK = 4
LIST_COL = 16


def tile_picked_ynewsfd_dup_p_kernel(
    tc, x_words, x_scales, w1, w2, e_words, e_scales, unit, age, offs, prv, art, mt, dup, out
):
    nc = tc.nc
    with ExitStack() as ctx:
        lists = ctx.enter_context(tc.tile_pool(name="lists", bufs=1))
        sb = ctx.enter_context(tc.tile_pool(name="sb", bufs=1))
        psum = ctx.enter_context(tc.psum_pool(name="psum", bufs=1))

        def load_list(src, name):
            tile = lists.tile([P, src.shape[1]], U16, name=name)
            nc.sync.dma_start(tile[:], src)
            return tile

        def entries(tile, first, count):
            return tile[:, first // LIST_COL : (first + count) // LIST_COL]

        def load_words(src, name):
            tile = sb.tile([P, T], U32, name=name)
            nc.sync.dma_start(tile[:].bitcast(I32), src[0].rearrange("p n t -> p (n t)").bitcast(I32))
            return tile

        def load_scales(src, name, queue):
            tile = sb.tile([P, T], U8, name=name)
            nc.vector.memset(tile[:].bitcast(I32), 0)
            for q in range(4):
                queue.dma_start(
                    tile[32 * q : 32 * q + 4, :].bitcast(I32), src[0, 4 * q : 4 * q + 4, :].bitcast(I32)
                )
            return tile

        def load_scales_staged(src, name):
            rows = sb.tile([P, T // 4], I32, name=name + "_rows")
            tile = sb.tile([P, T], U8, name=name)
            nc.vector.memset(tile[:].bitcast(I32), 0)
            for q in range(4):
                (nc.sync, nc.sync, nc.scalar, nc.scalar)[q].dma_start(rows[32 * q : 32 * q + 4, :], src[0, 4 * q : 4 * q + 4, :].bitcast(I32))
            for q in range(4):
                nc.vector.tensor_copy(tile[32 * q : 32 * q + 4, :].bitcast(I32), rows[32 * q : 32 * q + 4, :])
            return tile

        def load_weight(src, name):
            rows = src.rearrange("(p j) c -> p j c", j=PACK)
            parts = []
            for h in range(2):
                raw = sb.tile([P, PACK, H // 2], F32, name="%s_raw%d" % (name, h))
                nc.sync.dma_start(raw[:], rows[:, :, h * (H // 2) : (h + 1) * (H // 2)])
                parts.append(raw)
            return parts

        def gather(dtype, window, offsets, name, tag):
            picked = sb.tile([P, S], dtype, name=name, tag=tag, align_bytes=64)
            nc.vector.tensor_copy(picked[:], window[:].indirect(offsets[:]))
            return picked

        def deal_weight(parts, name, shares):
            dealt = sb.tile([P, PACK, P, PACK], BF16, name=name, tag="dealt", align_bytes=64)
            for copy, first, last in shares:
                h = first // 64
                copy(
                    dealt[:].rearrange("p t m j -> p m j t")[:, first:last],
                    parts[h][:].rearrange("p j (m t) -> p m j t", t=PACK)[:, first - 64 * h : last - 64 * h],
                )
            return dealt

        def quantize(values, width, name):
            codes = sb.tile([P, width], U32, name=name + "_codes", align_bytes=64)
            scales = sb.tile([P, width], U8, name=name + "_scales", align_bytes=64)
            nc.vector.quantize_mx(out=codes[:].bitcast(FP8X4), scales=scales[:], in_=values)
            return codes, scales

        def quantize_planes(dealt, name):
            first = quantize(dealt[:, 0].rearrange("p m j -> p (m j)"), P, name + "a")
            rest = quantize(dealt[:, 1:].rearrange("p t m j -> p (t m j)"), 3 * P, name + "b")
            planes = [(first[0][:], first[1][:])]
            for t in range(3):
                planes.append((rest[0][:, t * P : (t + 1) * P], rest[1][:, t * P : (t + 1) * P]))
            return planes

        def product(stationary, moving, tag):
            acc = psum.tile([P, S], F32, name=tag, tag=tag)
            nc.tensor.matmul_mx(
                out=acc[:],
                lhsT=stationary[0].bitcast(FP8X4),
                lhsT_scale=stationary[1],
                rhs=moving[0][:].bitcast(FP8X4),
                rhs_scale=moving[1][:],
                start=True,
                stop=True,
            )
            return acc

        offs_t = load_list(offs, "offs_t")
        xs = load_scales_staged(x_scales, "xs")
        xw = load_words(x_words, "xw")
        w1_raw = load_weight(w1, "w1")
        prv_t = load_list(prv, "prv_t")
        w2_raw = load_weight(w2, "w2")
        art_t = load_list(art, "art_t")
        es = load_scales(e_scales, "es", nc.sync)
        ew = load_words(e_words, "ew")
        mt_t = load_list(mt, "mt_t")
        unit_t = sb.tile([P, PACK], F32, name="unit_t")
        nc.sync.dma_start(unit_t[:], unit.rearrange("(p t) o -> p (t o)", t=PACK))
        age_t = sb.tile([P, T], F32, name="age_t")
        nc.sync.dma_start(age_t[:], age)
        dup_t = load_list(dup, "dup_t")

        xq_scales = gather(U8, xs, offs_t, "xq_scales", "xq_scales")
        xq_words = gather(U32, xw, offs_t, "xq_words", "xq_words")
        xq = (xq_words, xq_scales)
        w1_dealt = deal_weight(w1_raw, "w1_dealt", ((nc.scalar.copy, 0, 64), (nc.vector.tensor_copy, 64, 104), (nc.scalar.copy, 104, 128)))
        w1_planes = quantize_planes(w1_dealt, "w1q")
        y_ps = {t: product(w1_planes[t], xq, "bank%d" % t) for t in range(2)}
        w2_dealt = deal_weight(w2_raw, "w2_dealt", ((nc.vector.tensor_copy, 0, 64), (nc.vector.tensor_copy, 64, 128)))
        w2_planes = quantize_planes(w2_dealt, "w2q")
        yt_ps = [product(w2_planes[t], xq, "bank%d" % (2 + t)) for t in range(PACK)]

        y_sb, yp, th, nov, interest = {}, {}, {}, {}, {}

        def window_tile(width, spare, name):
            tile = sb.tile([P, width + spare], F32, name=name)
            nc.gpsimd.memset(tile[:, width:], 0.0)
            return tile

        def keep_y(t, on_vector):
            y_sb[t] = window_tile(S, 8, "y%d" % t)
            if on_vector:
                nc.vector.tensor_scalar(y_sb[t][:, :S], y_ps[t][:], 0.5, None, ALU.mult)
            else:
                nc.scalar.activation(y_sb[t][:, :S], y_ps[t][:], ACT.Copy, scale=0.5)

        def fetch_previous(t):
            yp[t] = sb.tile([P, S], F32, name="yp%d" % t, tag="yp%d" % t, align_bytes=64)
            nc.scalar.activation(yp[t][:], y_sb[t][:].indirect(prv_t[:]), ACT.Copy)

        def gate(t):
            th[t] = sb.tile([P, S], F32, name="th%d" % t, tag="th%d" % t, align_bytes=64)
            nc.scalar.activation(th[t][:], yt_ps[t][:], ACT.Tanh, scale=0.5)

        def novelty(t):
            nov[t] = sb.tile([P, S], F32, name="nov%d" % t)
            nc.vector.scalar_tensor_tensor(nov[t][:], yp[t][:], -0.5, y_sb[t][:, :S], ALU.mult, ALU.add)

        def gated(t):
            dw[t] = sb.tile([P, V, 2], F32, name="dw%d" % t, tag="dw%d" % t, align_bytes=64)
            nc.vector.scalar_tensor_tensor(
                dw[t][:].rearrange("p v d -> p (v d)"), th[t][:], 1.0, nov[t][:], ALU.add, ALU.mult
            )

        def pair_sum(t):
            interest[t] = window_tile(V, 8, "interest%d" % t)
            nc.vector.tensor_tensor(interest[t][:, :V], dw[t][:, :, 0], dw[t][:, :, 1], ALU.add)

        def fetch_mate(t, first, count):
            mate[t, first] = sb.tile([P, count], F32, name="mate%d_%d" % (t, first))
            nc.scalar.activation(mate[t, first][:], interest[t][:].indirect(entries(mt_t, first, count)), ACT.Copy)

        def compete(t, first, count, tag):
            soc[t, first] = sb.tile([P, count], F32, name="soc%d_%d" % (t, first), tag=tag, align_bytes=64)
            nc.vector.scalar_tensor_tensor(
                soc[t, first][:], mate[t, first][:], 0.8, interest[t][:, first : first + count], ALU.mult, ALU.max
            )

        dw, mate, soc = {}, {}, {}
        eq_scales = gather(U8, es, art_t, "eq_scales", "dealt")
        keep_y(0, False)
        fetch_previous(0)
        novelty(0)
        eq_words = gather(U32, ew, art_t, "eq_words", "yp0")
        keep_y(1, False)
        fetch_previous(1)
        novelty(1)
        gate(0)
        y_ps[2] = product(w1_planes[2], xq, "bank2")
        gate(1)
        y_ps[3] = product(w1_planes[3], xq, "bank3")
        gated(0)
        gated(1)
        keep_y(3, True)
        pair_sum(0)
        pair_sum(1)
        keep_y(2, False)
        fetch_previous(2)
        gate(2)
        fetch_previous(3)
        gate(3)
        novelty(2)
        gated(2)
        novelty(3)
        pair_sum(2)
        gated(3)
        pair_sum(3)
        hid_planes = sb.tile([P, PACK, V], BF16, name="hid_planes", tag="dw3", align_bytes=64)
        for t in range(3):
            fetch_mate(t, 0, V)
        for h in range(2):
            fetch_mate(3, h * P, P)
        for t in range(3):
            compete(t, 0, V, ("yp2", "yp3", "th3")[t])
        nc.vector.tensor_scalar(hid_planes[:, 2, :], soc[2, 0][:], unit_t[:, 2:3], None, ALU.mult)
        for t in range(2):
            nc.scalar.activation(hid_planes[:, t, :], soc[t, 0][:], ACT.Copy, scale=unit_t[:, t : t + 1])
        fade = sb.tile([P, S], F32, name="fade", tag="yp2", align_bytes=64)
        nc.scalar.activation(fade[:], age_t[:].indirect(art_t[:]), ACT.Exp, scale=-1.0)
        for h in range(2):
            compete(3, h * P, P, "soc3%d" % h)
        eq = (eq_words, eq_scales)
        sc = []
        for h in range(2):
            nc.vector.tensor_scalar(
                hid_planes[:, 3, h * P : (h + 1) * P], soc[3, h * P][:], unit_t[:, 3:4], None, ALU.mult
            )
            g = sb.tile([P, P, PACK], BF16, name="hid_grouped%d" % h, align_bytes=64)
            nc.vector.tensor_copy(
                g[:].rearrange("p (c i) t -> p c t i", i=4),
                hid_planes[:, :, h * P : (h + 1) * P].rearrange("p t (c i) -> p c t i", i=4),
            )
            hq = quantize(g[:].rearrange("p v t -> p (v t)"), P, "hq%d" % h)
            sc.append(product((hq[0][:], hq[1][:]), eq, "bank%d" % h))
        neg = []
        for h in range(2):
            n = sb.tile([P, S], F32, name="neg%d" % h)
            nc.vector.scalar_tensor_tensor(n[:], sc[h][:], -1.0, fade[:], ALU.mult, ALU.mult)
            neg.append(n)
        for h in range(2):
            for c in range(2):
                twin = sb.tile([P, 256], F32, name="twin%d%d" % (h, c))
                window = neg[h][:].indirect(entries(dup_t, c * 256, 256))
                if h == 1 and c == 0:
                    nc.vector.tensor_copy(twin[:], window)
                else:
                    nc.scalar.activation(twin[:], window, ACT.Copy)
                res = sb.tile([P, 256], F32, name="res%d%d" % (h, c))
                cols = slice(c * 256, (c + 1) * 256)
                nc.vector.scalar_tensor_tensor(res[:], twin[:], 0.0, neg[h][:, cols], ALU.min, ALU.subtract)
                nc.sync.dma_start(out[h * P : (h + 1) * P, cols], res[:])
